import numpy as np
import ml_dtypes


def mxq(x, axis, fmt="e4m3"):
    dtype, down = {"e4m3": (ml_dtypes.float8_e4m3fn, 7), "e5m2": (ml_dtypes.float8_e5m2, 14)}[fmt]
    v = np.moveaxis(np.asarray(x, np.float32).astype(ml_dtypes.bfloat16).astype(np.float64), axis, -1)
    blocks = v.reshape(v.shape[:-1] + (-1, 32))
    amax = np.abs(blocks).max(-1, keepdims=True)
    byte = np.maximum(np.where(amax > 0, np.frexp(amax)[1] - 1 + 127, 0) - down, 1)
    scale = np.exp2(byte - 127.0)
    codes = (blocks / scale).astype(np.float32).astype(dtype).astype(np.float64)
    return np.moveaxis((codes * scale).reshape(v.shape), -1, axis)


WIDE = False


def mx_kscale(k):
    if not WIDE:
        return np.ones(k)
    levels = np.array([10, -10, 5, -5, 0])
    if k % 512:
        return np.exp2(np.random.permutation(np.resize(levels, k // 32))).repeat(32)
    a = np.empty((k // 512, 16))
    for p in range(k // 512):
        a[p, :8] = np.random.permutation(np.resize(levels, 8))
        for g in range(8):
            far = levels[np.abs(levels - a[p, g]) >= 10]
            a[p, g + 8] = far[np.random.randint(len(far))]
    return np.exp2(a.ravel()).repeat(32)


def f64(x):
    return np.asarray(x).astype(np.float64)


def striped(idx):
    return np.tile(idx.reshape(-1, 16).T, (8, 1)).astype(np.uint16)


def unstriped(offs):
    return offs[:16].T.reshape(-1).astype(np.int64)


E2M1 = np.array([0.0, 0.5, 1.0, 1.5, 2.0, 3.0, 4.0, 6.0, -0.0, -0.5, -1.0, -1.5, -2.0, -3.0, -4.0, -6.0])


def pack_weight(w, fmt):
    k, n = w.shape
    w = f64(np.asarray(w, np.float32).astype(ml_dtypes.bfloat16)).reshape(k // 32, 32, n)
    amax = np.abs(w).max(1)
    if fmt == "e4m3":
        byte = np.frexp(amax)[1] - 1 + 127 - 7
    else:
        mant, ex = np.frexp(amax / 6.0)
        byte = np.where(mant > 0.5, ex, ex - 1) + 127
    byte = np.clip(np.where(amax > 0, byte, 1), 1, 254)
    scaled = (w * np.exp2(127.0 - byte)[:, None, :]).reshape(k, n).astype(np.float32)
    by_word = np.ascontiguousarray(scaled.reshape(k // 512, 128, 4, n).transpose(0, 1, 3, 2))
    if fmt == "e4m3":
        words = by_word.astype(ml_dtypes.float8_e4m3fn).view(np.uint8)
    else:
        c = by_word.astype(ml_dtypes.float4_e2m1fn).view(np.uint8) & 0xF
        words = (c[..., 0::2] | (c[..., 1::2] << 4)).reshape(k // 512, 128, 2 * n)
    return np.ascontiguousarray(words), np.ascontiguousarray(byte.astype(np.uint8).reshape(k // 512, 16, n))


def unpack_weight(words, scales, fmt):
    g, _, n = scales.shape
    words = np.ascontiguousarray(words).reshape(g, 128, n, -1)
    if fmt == "e4m3":
        vals = words.view(ml_dtypes.float8_e4m3fn).astype(np.float64)
    else:
        nib = np.empty((g, 128, n, 4), np.uint8)
        nib[..., 0::2] = words & 0xF
        nib[..., 1::2] = words >> 4
        vals = E2M1[nib]
    vals = vals * np.repeat(np.exp2(scales.astype(np.float64) - 127.0), 8, axis=1)[..., None]
    return vals.transpose(0, 1, 3, 2).reshape(g * 512, n)


K, T, E, C, N = 512, 512, 16, 128, 128
TOP = 4


def by_expert(wq, xq):
    return np.concatenate([wq[e].T @ xq[:, e * C:(e + 1) * C] for e in range(E)], axis=1)


def setup_inputs():
    n = np.random.standard_normal
    s = mx_kscale(K)[:, None]
    deal = np.repeat(np.arange(E), C).reshape(TOP, T)[:, np.random.permutation(T)]
    deal = np.take_along_axis(deal, np.argsort(np.random.rand(TOP, T), axis=0), axis=0)
    for _ in range(8):
        s_, t_ = np.random.permutation(T).reshape(2, -1); r = np.random.randint(TOP, size=T // 2); x, y = deal[r, s_].copy(), deal[r, t_].copy()
        ok = ~((deal[:, s_] == y).any(0) | (deal[:, t_] == x).any(0)); deal[r[ok], s_[ok]] = y[ok]; deal[r[ok], t_[ok]] = x[ok]
    order = np.lexsort((np.random.rand(TOP * T), deal.reshape(-1)))
    slot_token = order % T; pos = np.empty(TOP * T, np.int64); pos[order] = np.arange(TOP * T); pos = pos.reshape(TOP, T)
    g = np.random.uniform(0.5, 1.5, (TOP, T)); g = g / g.sum(0)
    w = [pack_weight(m, "e2m1") for m in n((E, K, N)) / np.sqrt(K) / s[None]]
    w_slot = np.empty(E * C)
    for r in range(TOP): w_slot[pos[r]] = g[r]
    return {
        "xT": (n((K, T)) * s).astype(np.float32),
        "w_words": np.stack([m[0] for m in w]),
        "w_scales": np.stack([m[1] for m in w]),
        "b": (0.3 * n((N, E))).astype(np.float32),
        "gate": np.tile(w_slot, (K, 1)).astype(np.float32),
        "offs": striped(slot_token),
        "pos1": striped(pos[0]),
        "pos2": striped(pos[1]),
        "pos3": striped(pos[2]),
        "pos4": striped(pos[3]),
    }


def reference(xT, w_words, w_scales, b, gate, offs, pos1, pos2, pos3, pos4):
    idx = unstriped(offs)
    w = np.stack([unpack_weight(w_words[e], w_scales[e], "e2m1") for e in range(E)])
    xq = mxq(f64(gate) * f64(xT)[:, idx], 0, "e4m3")
    y = by_expert(w, xq)
    y = y + np.repeat(f64(b), C, axis=1)
    return y[:, unstriped(pos1)] + y[:, unstriped(pos2)] + y[:, unstriped(pos3)] + y[:, unstriped(pos4)]

@@ -1,0 +1,123 @@
+from contextlib import ExitStack
+
+import concourse.mybir as mybir
+
+K, T, E, C, N = 512, 512, 16, 128, 128
+TOP = 4
+S = E * C
+P = 128
+PACK = 4
+FLOPS = 2 * K * N * S
+
+F32 = mybir.dt.float32
+BF16 = mybir.dt.bfloat16
+I32 = mybir.dt.int32
+U32 = mybir.dt.uint32
+U16 = mybir.dt.uint16
+U8 = mybir.dt.uint8
+FP8X4 = mybir.dt.float8_e4m3fn_x4
+FP4X4 = mybir.dt.float4_e2m1fn_x4
+MULT = mybir.AluOpType.mult
+ADD = mybir.AluOpType.add
+IDENTITY = mybir.ActivationFunctionType.Identity
+
+CHUNKS = [2, 2, 2, 2, 2, 2, 2, 1, 1]
+GATE_CUTS = [0, 256, 1024, 2048]
+HALF = T // 2
+
+
+def tile_moe_pre_lin_bias_kernel(tc, xT, w_words, w_scales, b, gate, offs, pos1, pos2, pos3, pos4, out):
+    nc = tc.nc
+    with ExitStack() as ctx:
+        lists = ctx.enter_context(tc.tile_pool(name="lists", bufs=1))
+        keep = ctx.enter_context(tc.tile_pool(name="keep", bufs=1))
+        ring = ctx.enter_context(tc.tile_pool(name="ring", bufs=3))
+        psum = ctx.enter_context(tc.psum_pool(name="psum", bufs=4))
+
+        w_plane = keep.tile([P, E * N], U8, name="w_plane", align_bytes=64)
+        nc.gpsimd.memset(w_plane[:].bitcast(I32), 0)
+
+        x_rows = xT.rearrange("(p j) t -> p j t", j=PACK)
+        x_planes = [keep.tile([P, T], F32, name="x_plane%d" % j) for j in range(PACK)]
+        gates = [keep.tile([P, GATE_CUTS[i + 1] - GATE_CUTS[i]], F32, name="gate%d" % i) for i in range(len(GATE_CUTS) - 1)]
+        offs_sb = lists.tile([P, S // 16], U16, name="offs_sb")
+        pos_sb = [lists.tile([P, T // 16], U16, name="pos_sb%d" % r) for r in range(TOP)]
+        w_sb = keep.tile([P, E * 2 * N], U8, name="w_sb", align_bytes=64)
+        bias = keep.tile([P, E], F32, name="bias")
+
+        def load_gate(i):
+            nc.sync.dma_start(out=gates[i][:], in_=gate[0:P, GATE_CUTS[i] : GATE_CUTS[i + 1]])
+
+        nc.sync.dma_start(out=x_planes[0][:], in_=x_rows[:, 0, :])
+        nc.sync.dma_start(offs_sb[:], offs)
+        load_gate(0)
+        for j in range(1, PACK):
+            nc.sync.dma_start(out=x_planes[j][:], in_=x_rows[:, j, :])
+        load_gate(1)
+        nc.sync.dma_start(
+            out=w_sb[:].bitcast(I32).rearrange("p (e c) -> p e c", e=E),
+            in_=w_words.bitcast(I32).rearrange("e a p c -> p (e a) c"),
+        )
+        scale_rows = w_scales.bitcast(I32).rearrange("e a q c -> q (e a) c")
+        plane_words = w_plane[:].bitcast(I32).rearrange("p (e c) -> p e c", e=E)
+        for quad in range(4):
+            nc.sync.dma_start(out=plane_words[32 * quad : 32 * quad + 4], in_=scale_rows[4 * quad : 4 * quad + 4])
+        nc.sync.dma_start(out=bias[:], in_=b)
+        load_gate(2)
+        for r, pos in enumerate((pos1, pos2, pos3, pos4)):
+            nc.sync.dma_start(pos_sb[r][:], pos)
+
+        y = keep.tile([P, S], F32, name="y")
+
+        e0 = 0
+        for n_exp in CHUNKS:
+            s0, width = e0 * C, n_exp * C
+            piece = max(i for i in range(len(gates)) if GATE_CUTS[i] <= s0)
+            gate_cols = gates[piece][:, s0 - GATE_CUTS[piece] : s0 - GATE_CUTS[piece] + width]
+            gathered = ring.tile([P, PACK * width], F32, name="gathered")
+            for j in range(PACK):
+                nc.vector.tensor_tensor(
+                    gathered[:, j * width : (j + 1) * width],
+                    x_planes[j][:].indirect(offs_sb[:, s0 // 16 : (s0 + width) // 16]),
+                    gate_cols,
+                    MULT,
+                )
+            woven = ring.tile([P, PACK * width], BF16, name="woven", align_bytes=64)
+            nc.scalar.copy(
+                out=woven[:].rearrange("p (c j) -> p c j", j=PACK),
+                in_=gathered[:].rearrange("p (j c) -> p c j", j=PACK),
+            )
+            codes = ring.tile([P, width], U32, name="codes", align_bytes=64)
+            scales = ring.tile([P, width], U8, name="scales", align_bytes=64)
+            nc.vector.quantize_mx(out=codes[:].bitcast(FP8X4), scales=scales[:], in_=woven[:])
+            acc = psum.tile([P, width], F32, name="acc")
+            for i in range(n_exp):
+                e = e0 + i
+                cols = slice(i * C, (i + 1) * C)
+                nc.tensor.matmul_mx(
+                    out=acc[:, cols],
+                    lhsT=w_sb[:, e * 2 * N : (e + 1) * 2 * N].bitcast(FP4X4),
+                    lhsT_scale=w_plane[:, e * N : (e + 1) * N],
+                    rhs=codes[:, cols].bitcast(FP8X4),
+                    rhs_scale=scales[:, cols],
+                    start=True,
+                    stop=True,
+                )
+            for i in range(n_exp):
+                e = e0 + i
+                nc.scalar.activation(out=y[:, e * C : (e + 1) * C], in_=acc[:, i * C : (i + 1) * C], func=IDENTITY, bias=bias[:, e : e + 1])
+            e0 += n_exp
+
+        halves = range(2)
+        sums = [None, None]
+        for r in range(TOP):
+            for h in halves:
+                window = y[:].indirect(pos_sb[r][:, h * HALF // 16 : (h + 1) * HALF // 16])
+                total = keep.tile([P, HALF], F32, name="sum%d_%d" % (r, h))
+                if r == 0:
+                    nc.vector.tensor_copy(total[:], window)
+                else:
+                    nc.vector.tensor_tensor(total[:], window, sums[h][:], ADD)
+                sums[h] = total
+        for h in halves:
+            nc.sync.dma_start(out=out[:, h * HALF : (h + 1) * HALF], in_=sums[h][:])

@@ -21,8 +21,10 @@ MULT = mybir.AluOpType.mult
 ADD = mybir.AluOpType.add
 IDENTITY = mybir.ActivationFunctionType.Identity
 
-CHUNKS = [2, 2, 2, 2, 2, 2, 2, 1, 1]
-GATE_CUTS = [0, 256, 1024, 2048]
+CHUNKS = [256, 512, 512, 384, 192, 128, 64]
+GATE_CUTS = [0, 256, 768, 1280, 2048]
+SPARE = 16
+PAIRS = [[(0, 256), (256, 512)]]
 HALF = T // 2
 
 
@@ -31,15 +33,16 @@ def tile_moe_pre_lin_bias_kernel(tc, xT, w_words, w_scales, b, gate, offs, pos1,
     with ExitStack() as ctx:
         lists = ctx.enter_context(tc.tile_pool(name="lists", bufs=1))
         keep = ctx.enter_context(tc.tile_pool(name="keep", bufs=1))
-        ring = ctx.enter_context(tc.tile_pool(name="ring", bufs=3))
+        ring = ctx.enter_context(tc.tile_pool(name="ring", bufs=2))
         psum = ctx.enter_context(tc.psum_pool(name="psum", bufs=4))
 
         w_plane = keep.tile([P, E * N], U8, name="w_plane", align_bytes=64)
-        nc.gpsimd.memset(w_plane[:].bitcast(I32), 0)
 
         x_rows = xT.rearrange("(p j) t -> p j t", j=PACK)
-        x_planes = [keep.tile([P, T], F32, name="x_plane%d" % j) for j in range(PACK)]
-        gates = [keep.tile([P, GATE_CUTS[i + 1] - GATE_CUTS[i]], F32, name="gate%d" % i) for i in range(len(GATE_CUTS) - 1)]
+        x_planes = [keep.tile([P, T + SPARE], F32, name="x_plane%d" % j) for j in range(PACK)]
+        for plane in x_planes:
+            nc.gpsimd.memset(plane[:, T:], 0.0)
+        gates = [keep.tile([P, GATE_CUTS[i + 1] - GATE_CUTS[i]], F32, name="gate%d" % i, tag="gate%d" % i, align_bytes=64) for i in range(len(GATE_CUTS) - 1)]
         offs_sb = lists.tile([P, S // 16], U16, name="offs_sb")
         pos_sb = [lists.tile([P, T // 16], U16, name="pos_sb%d" % r) for r in range(TOP)]
         w_sb = keep.tile([P, E * 2 * N], U8, name="w_sb", align_bytes=64)
@@ -48,11 +51,11 @@ def tile_moe_pre_lin_bias_kernel(tc, xT, w_words, w_scales, b, gate, offs, pos1,
         def load_gate(i):
             nc.sync.dma_start(out=gates[i][:], in_=gate[0:P, GATE_CUTS[i] : GATE_CUTS[i + 1]])
 
-        nc.sync.dma_start(out=x_planes[0][:], in_=x_rows[:, 0, :])
+        nc.sync.dma_start(out=x_planes[0][:, :T], in_=x_rows[:, 0, :])
         nc.sync.dma_start(offs_sb[:], offs)
         load_gate(0)
         for j in range(1, PACK):
-            nc.sync.dma_start(out=x_planes[j][:], in_=x_rows[:, j, :])
+            nc.sync.dma_start(out=x_planes[j][:, :T], in_=x_rows[:, j, :])
         load_gate(1)
         nc.sync.dma_start(
             out=w_sb[:].bitcast(I32).rearrange("p (e c) -> p e c", e=E),
@@ -63,17 +66,23 @@ def tile_moe_pre_lin_bias_kernel(tc, xT, w_words, w_scales, b, gate, offs, pos1,
         for quad in range(4):
             nc.sync.dma_start(out=plane_words[32 * quad : 32 * quad + 4], in_=scale_rows[4 * quad : 4 * quad + 4])
         nc.sync.dma_start(out=bias[:], in_=b)
-        load_gate(2)
+        for i in range(2, len(gates)):
+            load_gate(i)
         for r, pos in enumerate((pos1, pos2, pos3, pos4)):
             nc.sync.dma_start(pos_sb[r][:], pos)
 
         y = keep.tile([P, S], F32, name="y")
 
-        e0 = 0
-        for n_exp in CHUNKS:
-            s0, width = e0 * C, n_exp * C
+        scales = keep.tile([P, S], U8, name="scales", align_bytes=64)
+
+        s0 = 0
+        for c, width in enumerate(CHUNKS):
             piece = max(i for i in range(len(gates)) if GATE_CUTS[i] <= s0)
             gate_cols = gates[piece][:, s0 - GATE_CUTS[piece] : s0 - GATE_CUTS[piece] + width]
+            if s0 == GATE_CUTS[piece]:
+                tag = "gate%d" % (piece + 1) if piece == 1 else "codes%d" % piece
+                codes = keep.tile([P, GATE_CUTS[piece + 1] - s0], U32, name="codes%d" % piece, tag=tag, align_bytes=64)
+            base = GATE_CUTS[piece]
             gathered = ring.tile([P, PACK * width], F32, name="gathered")
             for j in range(PACK):
                 nc.vector.tensor_tensor(
@@ -84,40 +93,41 @@ def tile_moe_pre_lin_bias_kernel(tc, xT, w_words, w_scales, b, gate, offs, pos1,
                 )
             woven = ring.tile([P, PACK * width], BF16, name="woven", align_bytes=64)
             nc.scalar.copy(
-                out=woven[:].rearrange("p (c j) -> p c j", j=PACK),
-                in_=gathered[:].rearrange("p (j c) -> p c j", j=PACK),
+                out=woven[:].rearrange("p (c i j) -> p c j i", i=4, j=PACK),
+                in_=gathered[:].rearrange("p (j c i) -> p c j i", i=4, j=PACK),
             )
-            codes = ring.tile([P, width], U32, name="codes", align_bytes=64)
-            scales = ring.tile([P, width], U8, name="scales", align_bytes=64)
-            nc.vector.quantize_mx(out=codes[:].bitcast(FP8X4), scales=scales[:], in_=woven[:])
-            acc = psum.tile([P, width], F32, name="acc")
-            for i in range(n_exp):
-                e = e0 + i
-                cols = slice(i * C, (i + 1) * C)
+            done = 0
+            while done < width:
+                part = max(n for n in (64, 128, 256, 512) if n <= width - done)
+                cols = slice(s0 + done, s0 + done + part)
+                nc.vector.quantize_mx(out=codes[:, cols.start - base : cols.stop - base].bitcast(FP8X4), scales=scales[:, cols], in_=woven[:, PACK * done : PACK * (done + part)])
+                done += part
+            experts = range(s0 // C, (s0 + width) // C)
+            acc = psum.tile([P, len(experts) * C], F32, name="acc")
+            for i, e in enumerate(experts):
+                cols = slice(e * C, (e + 1) * C)
                 nc.tensor.matmul_mx(
-                    out=acc[:, cols],
+                    out=acc[:, i * C : (i + 1) * C],
                     lhsT=w_sb[:, e * 2 * N : (e + 1) * 2 * N].bitcast(FP4X4),
                     lhsT_scale=w_plane[:, e * N : (e + 1) * N],
-                    rhs=codes[:, cols].bitcast(FP8X4),
+                    rhs=codes[:, cols.start - base : cols.stop - base].bitcast(FP8X4),
                     rhs_scale=scales[:, cols],
                     start=True,
                     stop=True,
                 )
-            for i in range(n_exp):
-                e = e0 + i
+            for i, e in enumerate(experts):
                 nc.scalar.activation(out=y[:, e * C : (e + 1) * C], in_=acc[:, i * C : (i + 1) * C], func=IDENTITY, bias=bias[:, e : e + 1])
-            e0 += n_exp
+            s0 += width
 
-        halves = range(2)
-        sums = [None, None]
-        for r in range(TOP):
-            for h in halves:
-                window = y[:].indirect(pos_sb[r][:, h * HALF // 16 : (h + 1) * HALF // 16])
-                total = keep.tile([P, HALF], F32, name="sum%d_%d" % (r, h))
-                if r == 0:
-                    nc.vector.tensor_copy(total[:], window)
-                else:
-                    nc.vector.tensor_tensor(total[:], window, sums[h][:], ADD)
-                sums[h] = total
-        for h in halves:
-            nc.sync.dma_start(out=out[:, h * HALF : (h + 1) * HALF], in_=sums[h][:])
+        first = keep.tile([P, T], F32, name="first")
+        for h in range(2):
+            nc.vector.tensor_copy(first[:, h * HALF : (h + 1) * HALF], y[:].indirect(pos_sb[0][:, h * HALF // 16 : (h + 1) * HALF // 16]))
+        for pair in PAIRS:
+            sums = {t0: first[:, t0:t1] for t0, t1 in pair}
+            for r in range(1, TOP):
+                for t0, t1 in pair:
+                    total = keep.tile([P, t1 - t0], F32, name="sum%d_%d" % (r, t0))
+                    nc.vector.tensor_tensor(total[:], y[:].indirect(pos_sb[r][:, t0 // 16 : t1 // 16]), sums[t0], ADD)
+                    sums[t0] = total[:]
+            for t0, t1 in pair:
+                nc.sync.dma_start(out=out[:, t0:t1], in_=sums[t0])

@@ -21,11 +21,11 @@ MULT = mybir.AluOpType.mult
 ADD = mybir.AluOpType.add
 IDENTITY = mybir.ActivationFunctionType.Identity
 
-CHUNKS = [256, 512, 512, 384, 192, 128, 64]
-GATE_CUTS = [0, 256, 768, 1280, 2048]
-SPARE = 16
-PAIRS = [[(0, 256), (256, 512)]]
-HALF = T // 2
+BODY = [256, 384, 384, 384, 256]
+TAIL = [192, 128, 64]
+GATE_CUTS = [0, 256, 640, 1024, 2048]
+HALVES = [(0, 256), (256, 512)]
+LAST = [(0, 256), (256, 448), (448, 512)]
 
 
 def tile_moe_pre_lin_bias_kernel(tc, xT, w_words, w_scales, b, gate, offs, pos1, pos2, pos3, pos4, out):
@@ -37,11 +37,8 @@ def tile_moe_pre_lin_bias_kernel(tc, xT, w_words, w_scales, b, gate, offs, pos1,
         psum = ctx.enter_context(tc.psum_pool(name="psum", bufs=4))
 
         w_plane = keep.tile([P, E * N], U8, name="w_plane", align_bytes=64)
-
         x_rows = xT.rearrange("(p j) t -> p j t", j=PACK)
-        x_planes = [keep.tile([P, T + SPARE], F32, name="x_plane%d" % j) for j in range(PACK)]
-        for plane in x_planes:
-            nc.gpsimd.memset(plane[:, T:], 0.0)
+        x_planes = [keep.tile([P, T], F32, name="x_plane%d" % j) for j in range(PACK)]
         gates = [keep.tile([P, GATE_CUTS[i + 1] - GATE_CUTS[i]], F32, name="gate%d" % i, tag="gate%d" % i, align_bytes=64) for i in range(len(GATE_CUTS) - 1)]
         offs_sb = lists.tile([P, S // 16], U16, name="offs_sb")
         pos_sb = [lists.tile([P, T // 16], U16, name="pos_sb%d" % r) for r in range(TOP)]
@@ -51,11 +48,11 @@ def tile_moe_pre_lin_bias_kernel(tc, xT, w_words, w_scales, b, gate, offs, pos1,
         def load_gate(i):
             nc.sync.dma_start(out=gates[i][:], in_=gate[0:P, GATE_CUTS[i] : GATE_CUTS[i + 1]])
 
-        nc.sync.dma_start(out=x_planes[0][:, :T], in_=x_rows[:, 0, :])
+        nc.sync.dma_start(out=x_planes[0][:], in_=x_rows[:, 0, :])
         nc.sync.dma_start(offs_sb[:], offs)
         load_gate(0)
         for j in range(1, PACK):
-            nc.sync.dma_start(out=x_planes[j][:, :T], in_=x_rows[:, j, :])
+            nc.sync.dma_start(out=x_planes[j][:], in_=x_rows[:, j, :])
         load_gate(1)
         nc.sync.dma_start(
             out=w_sb[:].bitcast(I32).rearrange("p (e c) -> p e c", e=E),
@@ -72,17 +69,11 @@ def tile_moe_pre_lin_bias_kernel(tc, xT, w_words, w_scales, b, gate, offs, pos1,
             nc.sync.dma_start(pos_sb[r][:], pos)
 
         y = keep.tile([P, S], F32, name="y")
-
         scales = keep.tile([P, S], U8, name="scales", align_bytes=64)
 
-        s0 = 0
-        for c, width in enumerate(CHUNKS):
+        def gather(s0, width):
             piece = max(i for i in range(len(gates)) if GATE_CUTS[i] <= s0)
             gate_cols = gates[piece][:, s0 - GATE_CUTS[piece] : s0 - GATE_CUTS[piece] + width]
-            if s0 == GATE_CUTS[piece]:
-                tag = "gate%d" % (piece + 1) if piece == 1 else "codes%d" % piece
-                codes = keep.tile([P, GATE_CUTS[piece + 1] - s0], U32, name="codes%d" % piece, tag=tag, align_bytes=64)
-            base = GATE_CUTS[piece]
             gathered = ring.tile([P, PACK * width], F32, name="gathered")
             for j in range(PACK):
                 nc.vector.tensor_tensor(
@@ -91,43 +82,73 @@ def tile_moe_pre_lin_bias_kernel(tc, xT, w_words, w_scales, b, gate, offs, pos1,
                     gate_cols,
                     MULT,
                 )
-            woven = ring.tile([P, PACK * width], BF16, name="woven", align_bytes=64)
-            nc.scalar.copy(
-                out=woven[:].rearrange("p (c i j) -> p c j i", i=4, j=PACK),
+            return gathered
+
+        def weave(copy, woven, gathered):
+            copy(
+                out=woven.rearrange("p (c i j) -> p c j i", i=4, j=PACK),
                 in_=gathered[:].rearrange("p (j c i) -> p c j i", i=4, j=PACK),
             )
-            done = 0
-            while done < width:
-                part = max(n for n in (64, 128, 256, 512) if n <= width - done)
-                cols = slice(s0 + done, s0 + done + part)
-                nc.vector.quantize_mx(out=codes[:, cols.start - base : cols.stop - base].bitcast(FP8X4), scales=scales[:, cols], in_=woven[:, PACK * done : PACK * (done + part)])
-                done += part
-            experts = range(s0 // C, (s0 + width) // C)
-            acc = psum.tile([P, len(experts) * C], F32, name="acc")
+
+        def quantise(codes, s0, width, woven):
+            nc.vector.quantize_mx(out=codes.bitcast(FP8X4), scales=scales[:, s0 : s0 + width], in_=woven)
+
+        def multiply(acc, codes, experts):
             for i, e in enumerate(experts):
-                cols = slice(e * C, (e + 1) * C)
                 nc.tensor.matmul_mx(
                     out=acc[:, i * C : (i + 1) * C],
                     lhsT=w_sb[:, e * 2 * N : (e + 1) * 2 * N].bitcast(FP4X4),
                     lhsT_scale=w_plane[:, e * N : (e + 1) * N],
-                    rhs=codes[:, cols.start - base : cols.stop - base].bitcast(FP8X4),
-                    rhs_scale=scales[:, cols],
+                    rhs=codes[:, i * C : (i + 1) * C].bitcast(FP8X4),
+                    rhs_scale=scales[:, e * C : (e + 1) * C],
                     start=True,
                     stop=True,
                 )
             for i, e in enumerate(experts):
                 nc.scalar.activation(out=y[:, e * C : (e + 1) * C], in_=acc[:, i * C : (i + 1) * C], func=IDENTITY, bias=bias[:, e : e + 1])
+
+        s0 = 0
+        for c, width in enumerate(BODY):
+            gathered = gather(s0, width)
+            woven = ring.tile([P, PACK * width], BF16, name="woven", align_bytes=64)
+            weave(nc.scalar.copy, woven[:], gathered)
+            codes = keep.tile([P, width], U32, name="codes%d" % c, tag="gate2" if c == 1 else "codes%d" % c, align_bytes=64)
+            done = 0
+            while done < width:
+                part = max(n for n in (128, 256, 512) if n <= width - done)
+                quantise(codes[:, done : done + part], s0 + done, part, woven[:, PACK * done : PACK * (done + part)])
+                done += part
+            acc = psum.tile([P, width], F32, name="acc")
+            multiply(acc, codes, range(s0 // C, (s0 + width) // C))
             s0 += width
 
-        first = keep.tile([P, T], F32, name="first")
-        for h in range(2):
-            nc.vector.tensor_copy(first[:, h * HALF : (h + 1) * HALF], y[:].indirect(pos_sb[0][:, h * HALF // 16 : (h + 1) * HALF // 16]))
-        for pair in PAIRS:
-            sums = {t0: first[:, t0:t1] for t0, t1 in pair}
-            for r in range(1, TOP):
-                for t0, t1 in pair:
-                    total = keep.tile([P, t1 - t0], F32, name="sum%d_%d" % (r, t0))
-                    nc.vector.tensor_tensor(total[:], y[:].indirect(pos_sb[r][:, t0 // 16 : t1 // 16]), sums[t0], ADD)
-                    sums[t0] = total[:]
-            for t0, t1 in pair:
-                nc.sync.dma_start(out=out[:, t0:t1], in_=sums[t0])
+        tail0 = s0
+        tail_woven = keep.tile([P, PACK * (S - tail0)], BF16, name="tail_woven", align_bytes=64)
+
+        def finish(e):
+            codes = keep.tile([P, C], U32, name="tail_codes%d" % e, align_bytes=64)
+            at = PACK * (e * C - tail0)
+            quantise(codes[:], e * C, C, tail_woven[:, at : at + PACK * C])
+            acc = psum.tile([P, C], F32, name="tail_acc%d" % e, bufs=1)
+            multiply(acc, codes, [e])
+
+        for width in TAIL[:-1]:
+            gathered = gather(s0, width)
+            weave(nc.scalar.copy, tail_woven[:, PACK * (s0 - tail0) : PACK * (s0 - tail0 + width)], gathered)
+            s0 += width
+        gathered = gather(s0, TAIL[-1])
+        finish(E - 3)
+        weave(nc.vector.tensor_copy, tail_woven[:, PACK * (s0 - tail0) :], gathered)
+        finish(E - 2)
+        finish(E - 1)
+
+        sums = [keep.tile([P, T], F32, name="sum%d" % r) for r in range(TOP)]
+        for r in range(TOP):
+            for t0, t1 in LAST if r == TOP - 1 else HALVES:
+                picked = y[:].indirect(pos_sb[r][:, t0 // 16 : t1 // 16])
+                if r == 0:
+                    nc.vector.tensor_copy(sums[r][:, t0:t1], picked)
+                else:
+                    nc.vector.tensor_tensor(sums[r][:, t0:t1], picked, sums[r - 1][:, t0:t1], ADD)
+        for t0, t1 in LAST:
+            nc.sync.dma_start(out=out[:, t0:t1], in_=sums[TOP - 1][:, t0:t1])

from contextlib import ExitStack

import concourse.mybir as mybir

K, T, E, C, N = 512, 512, 16, 128, 128
TOP = 4
S = E * C
P = 128
PACK = 4
FLOPS = 2 * K * N * S

F32 = mybir.dt.float32
BF16 = mybir.dt.bfloat16
I32 = mybir.dt.int32
U32 = mybir.dt.uint32
U16 = mybir.dt.uint16
U8 = mybir.dt.uint8
FP8X4 = mybir.dt.float8_e4m3fn_x4
FP4X4 = mybir.dt.float4_e2m1fn_x4
MULT = mybir.AluOpType.mult
ADD = mybir.AluOpType.add
IDENTITY = mybir.ActivationFunctionType.Identity

BODY = [256, 384, 384, 384, 256]
TAIL = [192, 128, 64]
GATE_CUTS = [0, 256, 640, 1024, 2048]
HALVES = [(0, 256), (256, 512)]
LAST = [(0, 256), (256, 448), (448, 512)]


def tile_moe_pre_lin_bias_kernel(tc, xT, w_words, w_scales, b, gate, offs, pos1, pos2, pos3, pos4, out):
    nc = tc.nc
    with ExitStack() as ctx:
        lists = ctx.enter_context(tc.tile_pool(name="lists", bufs=1))
        keep = ctx.enter_context(tc.tile_pool(name="keep", bufs=1))
        ring = ctx.enter_context(tc.tile_pool(name="ring", bufs=2))
        psum = ctx.enter_context(tc.psum_pool(name="psum", bufs=4))

        w_plane = keep.tile([P, E * N], U8, name="w_plane", align_bytes=64)
        x_rows = xT.rearrange("(p j) t -> p j t", j=PACK)
        x_planes = [keep.tile([P, T], F32, name="x_plane%d" % j) for j in range(PACK)]
        gates = [keep.tile([P, GATE_CUTS[i + 1] - GATE_CUTS[i]], F32, name="gate%d" % i, tag="gate%d" % i, align_bytes=64) for i in range(len(GATE_CUTS) - 1)]
        offs_sb = lists.tile([P, S // 16], U16, name="offs_sb")
        pos_sb = [lists.tile([P, T // 16], U16, name="pos_sb%d" % r) for r in range(TOP)]
        w_sb = keep.tile([P, E * 2 * N], U8, name="w_sb", align_bytes=64)
        bias = keep.tile([P, E], F32, name="bias")

        def load_gate(i):
            nc.sync.dma_start(out=gates[i][:], in_=gate[0:P, GATE_CUTS[i] : GATE_CUTS[i + 1]])

        nc.sync.dma_start(out=x_planes[0][:], in_=x_rows[:, 0, :])
        nc.sync.dma_start(offs_sb[:], offs)
        load_gate(0)
        for j in range(1, PACK):
            nc.sync.dma_start(out=x_planes[j][:], in_=x_rows[:, j, :])
        load_gate(1)
        nc.sync.dma_start(
            out=w_sb[:].bitcast(I32).rearrange("p (e c) -> p e c", e=E),
            in_=w_words.bitcast(I32).rearrange("e a p c -> p (e a) c"),
        )
        scale_rows = w_scales.bitcast(I32).rearrange("e a q c -> q (e a) c")
        plane_words = w_plane[:].bitcast(I32).rearrange("p (e c) -> p e c", e=E)
        for quad in range(4):
            nc.sync.dma_start(out=plane_words[32 * quad : 32 * quad + 4], in_=scale_rows[4 * quad : 4 * quad + 4])
        nc.sync.dma_start(out=bias[:], in_=b)
        for i in range(2, len(gates)):
            load_gate(i)
        for r, pos in enumerate((pos1, pos2, pos3, pos4)):
            nc.sync.dma_start(pos_sb[r][:], pos)

        y = keep.tile([P, S], F32, name="y")
        scales = keep.tile([P, S], U8, name="scales", align_bytes=64)

        def gather(s0, width):
            piece = max(i for i in range(len(gates)) if GATE_CUTS[i] <= s0)
            gate_cols = gates[piece][:, s0 - GATE_CUTS[piece] : s0 - GATE_CUTS[piece] + width]
            gathered = ring.tile([P, PACK * width], F32, name="gathered")
            for j in range(PACK):
                nc.vector.tensor_tensor(
                    gathered[:, j * width : (j + 1) * width],
                    x_planes[j][:].indirect(offs_sb[:, s0 // 16 : (s0 + width) // 16]),
                    gate_cols,
                    MULT,
                )
            return gathered

        def weave(copy, woven, gathered):
            copy(
                out=woven.rearrange("p (c i j) -> p c j i", i=4, j=PACK),
                in_=gathered[:].rearrange("p (j c i) -> p c j i", i=4, j=PACK),
            )

        def quantise(codes, s0, width, woven):
            nc.vector.quantize_mx(out=codes.bitcast(FP8X4), scales=scales[:, s0 : s0 + width], in_=woven)

        def multiply(acc, codes, experts):
            for i, e in enumerate(experts):
                nc.tensor.matmul_mx(
                    out=acc[:, i * C : (i + 1) * C],
                    lhsT=w_sb[:, e * 2 * N : (e + 1) * 2 * N].bitcast(FP4X4),
                    lhsT_scale=w_plane[:, e * N : (e + 1) * N],
                    rhs=codes[:, i * C : (i + 1) * C].bitcast(FP8X4),
                    rhs_scale=scales[:, e * C : (e + 1) * C],
                    start=True,
                    stop=True,
                )
            for i, e in enumerate(experts):
                nc.scalar.activation(out=y[:, e * C : (e + 1) * C], in_=acc[:, i * C : (i + 1) * C], func=IDENTITY, bias=bias[:, e : e + 1])

        s0 = 0
        for c, width in enumerate(BODY):
            gathered = gather(s0, width)
            woven = ring.tile([P, PACK * width], BF16, name="woven", align_bytes=64)
            weave(nc.scalar.copy, woven[:], gathered)
            codes = keep.tile([P, width], U32, name="codes%d" % c, tag="gate2" if c == 1 else "codes%d" % c, align_bytes=64)
            done = 0
            while done < width:
                part = max(n for n in (128, 256, 512) if n <= width - done)
                quantise(codes[:, done : done + part], s0 + done, part, woven[:, PACK * done : PACK * (done + part)])
                done += part
            acc = psum.tile([P, width], F32, name="acc")
            multiply(acc, codes, range(s0 // C, (s0 + width) // C))
            s0 += width

        tail0 = s0
        tail_woven = keep.tile([P, PACK * (S - tail0)], BF16, name="tail_woven", align_bytes=64)

        def finish(e):
            codes = keep.tile([P, C], U32, name="tail_codes%d" % e, align_bytes=64)
            at = PACK * (e * C - tail0)
            quantise(codes[:], e * C, C, tail_woven[:, at : at + PACK * C])
            acc = psum.tile([P, C], F32, name="tail_acc%d" % e, bufs=1)
            multiply(acc, codes, [e])

        for width in TAIL[:-1]:
            gathered = gather(s0, width)
            weave(nc.scalar.copy, tail_woven[:, PACK * (s0 - tail0) : PACK * (s0 - tail0 + width)], gathered)
            s0 += width
        gathered = gather(s0, TAIL[-1])
        finish(E - 3)
        weave(nc.vector.tensor_copy, tail_woven[:, PACK * (s0 - tail0) :], gathered)
        finish(E - 2)
        finish(E - 1)

        sums = [keep.tile([P, T], F32, name="sum%d" % r) for r in range(TOP)]
        for r in range(TOP):
            for t0, t1 in LAST if r == TOP - 1 else HALVES:
                picked = y[:].indirect(pos_sb[r][:, t0 // 16 : t1 // 16])
                if r == 0:
                    nc.vector.tensor_copy(sums[r][:, t0:t1], picked)
                else:
                    nc.vector.tensor_tensor(sums[r][:, t0:t1], picked, sums[r - 1][:, t0:t1], ADD)
        for t0, t1 in LAST:
            nc.sync.dma_start(out=out[:, t0:t1], in_=sums[TOP - 1][:, t0:t1])
